import numpy as np
import ml_dtypes

BF16 = ml_dtypes.bfloat16


def bf(x):
    return np.asarray(x, np.float32).astype(BF16)


def f32(x):
    return np.asarray(x, np.float32)


def f64(x):
    return np.asarray(x).astype(np.float64)


def striped(idx):
    return np.tile(idx.reshape(-1, 16).T, (8, 1))


S, K, M, N, T, D = 512, 128, 256, 384, 256, 128


def setup_inputs():
    return {"base": bf(np.random.standard_normal((M, S))), "q": bf(1.5 * np.random.standard_normal((K, N)) / np.sqrt(K)), "k": bf(np.random.standard_normal((K, T))), "v": bf(np.random.standard_normal((T, D))), "w": bf(2.0 * np.random.standard_normal((D, M)) / np.sqrt(D)), "r": f32(0.7 * np.random.standard_normal((1, T))), "offs": striped(np.random.permutation(S)[:N])}


def reference(base, q, k, v, w, r, offs):
    idx = offs[:16].T.reshape(-1)
    a = f64(q).T @ f64(k) + f64(r)
    a = np.exp(a - a.max(axis=1, keepdims=True))
    a = a / a.sum(axis=1, keepdims=True)
    z = f64(base).copy()
    z[:, idx] += f64(w).T @ (a @ f64(v)).T
    return z

@@ -1,0 +1,98 @@
+import concourse.mybir as mybir
+from concourse.masks import make_identity
+
+BF16, F32, U16 = mybir.dt.bfloat16, mybir.dt.float32, mybir.dt.uint16
+EXP = mybir.ActivationFunctionType.Exp
+MAX, MULT = mybir.AluOpType.max, mybir.AluOpType.mult
+AXIS_X = mybir.AxisListType.X
+
+P = 128
+S, K, M, N, T, D = 512, 128, 256, 384, 256, 128
+JB, TB, MB = N // P, T // P, M // P
+R_ROWS = 32
+FLOPS = 2 * (N * K * T + N * T * D + N * D * M)
+
+
+def tile_rows_attnback_kernel(tc, base, q, k, v, w, r, offs, out):
+    nc = tc.nc
+    with (
+        tc.tile_pool(name="held", bufs=1) as held,
+        tc.tile_pool(name="work", bufs=JB) as work,
+        tc.psum_pool(name="psum_one", bufs=1) as psum_one,
+        tc.psum_pool(name="psum_scores", bufs=JB) as psum_scores,
+    ):
+        offsets = held.tile([P, N // 16], U16, name="offsets")
+        base_sb = held.tile([P, MB, S], BF16, name="base_sb")
+        q_sb = held.tile([P, N], BF16, name="q_sb")
+        k_sb = held.tile([P, T], BF16, name="k_sb")
+        v_sb = held.tile([P, TB, D], BF16, name="v_sb")
+        w_sb = held.tile([P, M], BF16, name="w_sb")
+        r_rows = held.tile([R_ROWS, T], F32, name="r_rows")
+
+        nc.sync.dma_start(q_sb[:], q)
+        nc.scalar.dma_start(r_rows[:], r.rearrange("o t -> (o t)").partition_broadcast(R_ROWS))
+        nc.sync.dma_start(k_sb[:], k)
+        nc.sync.dma_start(base_sb[:], base.rearrange("(a p) s -> p a s", p=P))
+        nc.scalar.dma_start(v_sb[:], v.rearrange("(a p) d -> p a d", p=P))
+        nc.scalar.dma_start(w_sb[:], w)
+        nc.sync.dma_start(offsets[:], offs)
+
+        early = held.tile([P, 1], F32, name="early")
+        nc.vector.memset(early[:], 0.0)
+        nc.scalar.activation(early[:], early[:], EXP)
+
+        r_weights = held.tile([R_ROWS, P], F32, name="r_weights")
+        nc.vector.memset(r_weights[:], 1.0 / R_ROWS)
+        ones = held.tile([P, P], BF16, name="ones")
+        nc.vector.memset(ones[:], 1.0)
+        ident = held.tile([P, P], BF16, name="ident")
+        make_identity(nc, ident[:])
+
+        scores = [psum_scores.tile([P, T], F32, name=f"scores{b}", tag="scores") for b in range(JB)]
+        for b in range(JB):
+            nc.tensor.matmul(scores[b][:], r_weights[:], r_rows[:], start=True, stop=False)
+            nc.tensor.matmul(scores[b][:], q_sb[:, b * P : (b + 1) * P], k_sb[:], start=False, stop=True)
+
+        windows = [psum_one.tile([P, S], F32, name=f"window{m}") for m in range(MB)]
+        for m in range(MB):
+            nc.tensor.matmul(windows[m][:], ident[:], base_sb[:, m, :], start=True, stop=False)
+
+        o_psum = psum_one.tile([P, N], F32, name="o_psum")
+        inverses = []
+        for b in range(JB):
+            neg_max = work.tile([P, 1], F32, name="neg_max")
+            nc.vector.tensor_reduce(neg_max[:], scores[b][:], AXIS_X, MAX, negate=True)
+            e = work.tile([P, T], BF16, name="e")
+            nc.scalar.activation(e[:], scores[b][:], EXP, bias=neg_max[:])
+
+            e_t_psum = psum_one.tile([P, TB, P], BF16, name="e_t_psum")
+            for t in range(TB):
+                nc.tensor.transpose(e_t_psum[:, t, :], e[:, t * P : (t + 1) * P], ident[:])
+            e_t = work.tile([P, TB, P], BF16, name="e_t")
+            nc.vector.tensor_copy(e_t[:], e_t_psum[:])
+
+            sums = psum_one.tile([P, P], F32, name="sums")
+            for t in range(TB):
+                nc.tensor.matmul(sums[:], ones[:], e_t[:, t, :], start=t == 0, stop=t == TB - 1)
+            for t in range(TB):
+                nc.tensor.matmul(o_psum[:, b * P : (b + 1) * P], v_sb[:, t, :], e_t[:, t, :],
+                                 start=t == 0, stop=t == TB - 1)
+            inverse = work.tile([P, P], F32, name="inverse")
+            nc.vector.reciprocal(inverse[:], sums[:])
+            inverses.append(inverse)
+
+        for b in range(JB):
+            o = work.tile([P, P], BF16, name="o")
+            nc.vector.tensor_tensor(o[:], o_psum[:, b * P : (b + 1) * P], inverses[b][:], MULT)
+            places = offsets[:, b * (P // 16) : (b + 1) * (P // 16)]
+            for m in range(MB):
+                nc.tensor.matmul(windows[m][:].indirect(places), w_sb[:, m * P : (m + 1) * P], o[:],
+                                 start=False, stop=b == JB - 1)
+
+        for m in range(MB):
+            z = held.tile([P, S], F32, name=f"z{m}")
+            if m == 0:
+                nc.vector.tensor_copy(z[:], windows[m][:])
+            else:
+                nc.scalar.copy(z[:], windows[m][:])
+            nc.sync.dma_start(out[m * P : (m + 1) * P, :], z[:])

@@ -10,6 +10,7 @@ P = 128
 S, K, M, N, T, D = 512, 128, 256, 384, 256, 128
 JB, TB, MB = N // P, T // P, M // P
 R_ROWS = 32
+WARM_UPS = 5
 FLOPS = 2 * (N * K * T + N * T * D + N * D * M)
 
 
@@ -29,13 +30,19 @@ def tile_rows_attnback_kernel(tc, base, q, k, v, w, r, offs, out):
         w_sb = held.tile([P, M], BF16, name="w_sb")
         r_rows = held.tile([R_ROWS, T], F32, name="r_rows")
 
-        nc.sync.dma_start(q_sb[:], q)
-        nc.scalar.dma_start(r_rows[:], r.rearrange("o t -> (o t)").partition_broadcast(R_ROWS))
+        nc.sync.dma_start(r_rows[:], r.rearrange("o t -> (o t)").partition_broadcast(R_ROWS))
+        nc.scalar.dma_start(q_sb[:], q)
         nc.sync.dma_start(k_sb[:], k)
         nc.sync.dma_start(base_sb[:], base.rearrange("(a p) s -> p a s", p=P))
         nc.scalar.dma_start(v_sb[:], v.rearrange("(a p) d -> p a d", p=P))
         nc.scalar.dma_start(w_sb[:], w)
         nc.sync.dma_start(offsets[:], offs)
+
+        zeros = held.tile([P, S], BF16, name="zeros")
+        nc.vector.memset(zeros[:], 0.0)
+        spare = psum_one.tile([P, S], F32, name="spare", tag="sums")
+        for warm_up in range(WARM_UPS):
+            nc.tensor.matmul(spare[:], zeros[:, :P], zeros[:], start=True, stop=True)
 
         early = held.tile([P, 1], F32, name="early")
         nc.vector.memset(early[:], 0.0)
@@ -71,7 +78,7 @@ def tile_rows_attnback_kernel(tc, base, q, k, v, w, r, offs, out):
             e_t = work.tile([P, TB, P], BF16, name="e_t")
             nc.vector.tensor_copy(e_t[:], e_t_psum[:])
 
-            sums = psum_one.tile([P, P], F32, name="sums")
+            sums = psum_one.tile([P, P], F32, name="sums", tag="sums")
             for t in range(TB):
                 nc.tensor.matmul(sums[:], ones[:], e_t[:, t, :], start=t == 0, stop=t == TB - 1)
             for t in range(TB):

@@ -3,14 +3,13 @@ from concourse.masks import make_identity
 
 BF16, F32, U16 = mybir.dt.bfloat16, mybir.dt.float32, mybir.dt.uint16
 EXP = mybir.ActivationFunctionType.Exp
-MAX, MULT = mybir.AluOpType.max, mybir.AluOpType.mult
+ADD, MAX, MULT = mybir.AluOpType.add, mybir.AluOpType.max, mybir.AluOpType.mult
 AXIS_X = mybir.AxisListType.X
 
 P = 128
 S, K, M, N, T, D = 512, 128, 256, 384, 256, 128
 JB, TB, MB = N // P, T // P, M // P
-R_ROWS = 32
-WARM_UPS = 5
+WARM_UPS = 3
 FLOPS = 2 * (N * K * T + N * T * D + N * D * M)
 
 
@@ -20,7 +19,7 @@ def tile_rows_attnback_kernel(tc, base, q, k, v, w, r, offs, out):
         tc.tile_pool(name="held", bufs=1) as held,
         tc.tile_pool(name="work", bufs=JB) as work,
         tc.psum_pool(name="psum_one", bufs=1) as psum_one,
-        tc.psum_pool(name="psum_scores", bufs=JB) as psum_scores,
+        tc.psum_pool(name="psum_two", bufs=2) as psum_two,
     ):
         offsets = held.tile([P, N // 16], U16, name="offsets")
         base_sb = held.tile([P, MB, S], BF16, name="base_sb")
@@ -28,11 +27,11 @@ def tile_rows_attnback_kernel(tc, base, q, k, v, w, r, offs, out):
         k_sb = held.tile([P, T], BF16, name="k_sb")
         v_sb = held.tile([P, TB, D], BF16, name="v_sb")
         w_sb = held.tile([P, M], BF16, name="w_sb")
-        r_rows = held.tile([R_ROWS, T], F32, name="r_rows")
+        r_sb = held.tile([P, T], F32, name="r_sb")
 
-        nc.sync.dma_start(r_rows[:], r.rearrange("o t -> (o t)").partition_broadcast(R_ROWS))
-        nc.scalar.dma_start(q_sb[:], q)
+        nc.sync.dma_start(q_sb[:], q)
         nc.sync.dma_start(k_sb[:], k)
+        nc.scalar.dma_start(r_sb[:], r.rearrange("o t -> (o t)").partition_broadcast(P))
         nc.sync.dma_start(base_sb[:], base.rearrange("(a p) s -> p a s", p=P))
         nc.scalar.dma_start(v_sb[:], v.rearrange("(a p) d -> p a d", p=P))
         nc.scalar.dma_start(w_sb[:], w)
@@ -40,7 +39,7 @@ def tile_rows_attnback_kernel(tc, base, q, k, v, w, r, offs, out):
 
         zeros = held.tile([P, S], BF16, name="zeros")
         nc.vector.memset(zeros[:], 0.0)
-        spare = psum_one.tile([P, S], F32, name="spare", tag="sums")
+        spare = psum_two.tile([P, S], F32, name="spare", tag="o_psum")
         for warm_up in range(WARM_UPS):
             nc.tensor.matmul(spare[:], zeros[:, :P], zeros[:], start=True, stop=True)
 
@@ -48,53 +47,46 @@ def tile_rows_attnback_kernel(tc, base, q, k, v, w, r, offs, out):
         nc.vector.memset(early[:], 0.0)
         nc.scalar.activation(early[:], early[:], EXP)
 
-        r_weights = held.tile([R_ROWS, P], F32, name="r_weights")
-        nc.vector.memset(r_weights[:], 1.0 / R_ROWS)
-        ones = held.tile([P, P], BF16, name="ones")
-        nc.vector.memset(ones[:], 1.0)
         ident = held.tile([P, P], BF16, name="ident")
         make_identity(nc, ident[:])
 
-        scores = [psum_scores.tile([P, T], F32, name=f"scores{b}", tag="scores") for b in range(JB)]
+        p_blocks = []
         for b in range(JB):
-            nc.tensor.matmul(scores[b][:], r_weights[:], r_rows[:], start=True, stop=False)
-            nc.tensor.matmul(scores[b][:], q_sb[:, b * P : (b + 1) * P], k_sb[:], start=False, stop=True)
+            scores = psum_two.tile([P, T], F32, name="scores")
+            nc.tensor.matmul(scores[:], q_sb[:, b * P : (b + 1) * P], k_sb[:], start=True, stop=True)
+            a = work.tile([P, T], F32, name="a")
+            nc.vector.tensor_tensor(a[:], scores[:], r_sb[:], ADD)
+            neg_max = work.tile([P, 1], F32, name="neg_max")
+            nc.vector.tensor_reduce(neg_max[:], a[:], AXIS_X, MAX, negate=True)
+            e = work.tile([P, T], F32, name="e")
+            total = work.tile([P, 1], F32, name="total")
+            nc.scalar.activation(e[:], a[:], EXP, bias=neg_max[:], accum_out=total[:])
+            inverse = work.tile([P, 1], F32, name="inverse")
+            nc.vector.reciprocal(inverse[:], total[:])
+            p = work.tile([P, T], BF16, name="p")
+            nc.vector.tensor_scalar(p[:], e[:], inverse[:], None, MULT)
+            p_blocks.append(p)
 
         windows = [psum_one.tile([P, S], F32, name=f"window{m}") for m in range(MB)]
         for m in range(MB):
             nc.tensor.matmul(windows[m][:], ident[:], base_sb[:, m, :], start=True, stop=False)
 
-        o_psum = psum_one.tile([P, N], F32, name="o_psum")
-        inverses = []
+        o = held.tile([P, N], BF16, name="o")
         for b in range(JB):
-            neg_max = work.tile([P, 1], F32, name="neg_max")
-            nc.vector.tensor_reduce(neg_max[:], scores[b][:], AXIS_X, MAX, negate=True)
-            e = work.tile([P, T], BF16, name="e")
-            nc.scalar.activation(e[:], scores[b][:], EXP, bias=neg_max[:])
-
-            e_t_psum = psum_one.tile([P, TB, P], BF16, name="e_t_psum")
+            p_t_psum = psum_two.tile([P, TB, P], BF16, name="p_t_psum")
             for t in range(TB):
-                nc.tensor.transpose(e_t_psum[:, t, :], e[:, t * P : (t + 1) * P], ident[:])
-            e_t = work.tile([P, TB, P], BF16, name="e_t")
-            nc.vector.tensor_copy(e_t[:], e_t_psum[:])
+                nc.tensor.transpose(p_t_psum[:, t, :], p_blocks[b][:, t * P : (t + 1) * P], ident[:])
+            p_t = work.tile([P, TB, P], BF16, name="p_t")
+            nc.scalar.copy(p_t[:], p_t_psum[:])
 
-            sums = psum_one.tile([P, P], F32, name="sums", tag="sums")
+            o_psum = psum_two.tile([P, P], F32, name="o_psum", tag="o_psum")
             for t in range(TB):
-                nc.tensor.matmul(sums[:], ones[:], e_t[:, t, :], start=t == 0, stop=t == TB - 1)
-            for t in range(TB):
-                nc.tensor.matmul(o_psum[:, b * P : (b + 1) * P], v_sb[:, t, :], e_t[:, t, :],
-                                 start=t == 0, stop=t == TB - 1)
-            inverse = work.tile([P, P], F32, name="inverse")
-            nc.vector.reciprocal(inverse[:], sums[:])
-            inverses.append(inverse)
+                nc.tensor.matmul(o_psum[:], v_sb[:, t, :], p_t[:, t, :], start=t == 0, stop=t == TB - 1)
+            nc.vector.tensor_copy(o[:, b * P : (b + 1) * P], o_psum[:])
 
-        for b in range(JB):
-            o = work.tile([P, P], BF16, name="o")
-            nc.vector.tensor_tensor(o[:], o_psum[:, b * P : (b + 1) * P], inverses[b][:], MULT)
-            places = offsets[:, b * (P // 16) : (b + 1) * (P // 16)]
-            for m in range(MB):
-                nc.tensor.matmul(windows[m][:].indirect(places), w_sb[:, m * P : (m + 1) * P], o[:],
-                                 start=False, stop=b == JB - 1)
+        for m in range(MB):
+            nc.tensor.matmul(windows[m][:].indirect(offsets[:]), w_sb[:, m * P : (m + 1) * P], o[:],
+                             start=False, stop=True)
 
         for m in range(MB):
             z = held.tile([P, S], F32, name=f"z{m}")

@@ -3,13 +3,13 @@ from concourse.masks import make_identity
 
 BF16, F32, U16 = mybir.dt.bfloat16, mybir.dt.float32, mybir.dt.uint16
 EXP = mybir.ActivationFunctionType.Exp
-ADD, MAX, MULT = mybir.AluOpType.add, mybir.AluOpType.max, mybir.AluOpType.mult
+MAX, MULT = mybir.AluOpType.max, mybir.AluOpType.mult
 AXIS_X = mybir.AxisListType.X
 
 P = 128
 S, K, M, N, T, D = 512, 128, 256, 384, 256, 128
 JB, TB, MB = N // P, T // P, M // P
-WARM_UPS = 3
+WARM_UPS = 5
 FLOPS = 2 * (N * K * T + N * T * D + N * D * M)
 
 
@@ -18,7 +18,7 @@ def tile_rows_attnback_kernel(tc, base, q, k, v, w, r, offs, out):
     with (
         tc.tile_pool(name="held", bufs=1) as held,
         tc.tile_pool(name="work", bufs=JB) as work,
-        tc.psum_pool(name="psum_one", bufs=1) as psum_one,
+        tc.psum_pool(name="psum_three", bufs=JB) as psum_three,
         tc.psum_pool(name="psum_two", bufs=2) as psum_two,
     ):
         offsets = held.tile([P, N // 16], U16, name="offsets")
@@ -27,19 +27,19 @@ def tile_rows_attnback_kernel(tc, base, q, k, v, w, r, offs, out):
         k_sb = held.tile([P, T], BF16, name="k_sb")
         v_sb = held.tile([P, TB, D], BF16, name="v_sb")
         w_sb = held.tile([P, M], BF16, name="w_sb")
-        r_sb = held.tile([P, T], F32, name="r_sb")
+        r_row = held.tile([1, T], F32, name="r_row")
 
+        nc.sync.dma_start(r_row[:], r)
         nc.sync.dma_start(q_sb[:], q)
         nc.sync.dma_start(k_sb[:], k)
-        nc.scalar.dma_start(r_sb[:], r.rearrange("o t -> (o t)").partition_broadcast(P))
+        nc.sync.dma_start(v_sb[:], v.rearrange("(a p) d -> p a d", p=P))
         nc.sync.dma_start(base_sb[:], base.rearrange("(a p) s -> p a s", p=P))
-        nc.scalar.dma_start(v_sb[:], v.rearrange("(a p) d -> p a d", p=P))
-        nc.scalar.dma_start(w_sb[:], w)
+        nc.sync.dma_start(w_sb[:], w)
         nc.sync.dma_start(offsets[:], offs)
 
         zeros = held.tile([P, S], BF16, name="zeros")
         nc.vector.memset(zeros[:], 0.0)
-        spare = psum_two.tile([P, S], F32, name="spare", tag="o_psum")
+        spare = psum_three.tile([P, S], F32, name="spare", tag="o_psum")
         for warm_up in range(WARM_UPS):
             nc.tensor.matmul(spare[:], zeros[:, :P], zeros[:], start=True, stop=True)
 
@@ -47,42 +47,45 @@ def tile_rows_attnback_kernel(tc, base, q, k, v, w, r, offs, out):
         nc.vector.memset(early[:], 0.0)
         nc.scalar.activation(early[:], early[:], EXP)
 
+        ones_row = held.tile([1, P], F32, name="ones_row")
+        nc.vector.memset(ones_row[:], 1.0)
         ident = held.tile([P, P], BF16, name="ident")
         make_identity(nc, ident[:])
 
-        p_blocks = []
+        e_blocks, totals = [], []
         for b in range(JB):
-            scores = psum_two.tile([P, T], F32, name="scores")
-            nc.tensor.matmul(scores[:], q_sb[:, b * P : (b + 1) * P], k_sb[:], start=True, stop=True)
-            a = work.tile([P, T], F32, name="a")
-            nc.vector.tensor_tensor(a[:], scores[:], r_sb[:], ADD)
+            a = psum_three.tile([P, T], F32, name="a")
+            nc.tensor.matmul(a[:], ones_row[:], r_row[:], start=True, stop=False)
+            nc.tensor.matmul(a[:], q_sb[:, b * P : (b + 1) * P], k_sb[:], start=False, stop=True)
             neg_max = work.tile([P, 1], F32, name="neg_max")
             nc.vector.tensor_reduce(neg_max[:], a[:], AXIS_X, MAX, negate=True)
             e = work.tile([P, T], F32, name="e")
+            e_blocks.append(e)
             total = work.tile([P, 1], F32, name="total")
             nc.scalar.activation(e[:], a[:], EXP, bias=neg_max[:], accum_out=total[:])
-            inverse = work.tile([P, 1], F32, name="inverse")
-            nc.vector.reciprocal(inverse[:], total[:])
-            p = work.tile([P, T], BF16, name="p")
-            nc.vector.tensor_scalar(p[:], e[:], inverse[:], None, MULT)
-            p_blocks.append(p)
-
-        windows = [psum_one.tile([P, S], F32, name=f"window{m}") for m in range(MB)]
-        for m in range(MB):
-            nc.tensor.matmul(windows[m][:], ident[:], base_sb[:, m, :], start=True, stop=False)
+            totals.append(total)
 
         o = held.tile([P, N], BF16, name="o")
         for b in range(JB):
-            p_t_psum = psum_two.tile([P, TB, P], BF16, name="p_t_psum")
+            inverse = work.tile([P, 1], F32, name="inverse")
+            nc.vector.reciprocal(inverse[:], totals[b][:])
+            p = work.tile([P, T], BF16, name="p")
+            nc.vector.tensor_scalar(p[:], e_blocks[b][:], inverse[:], None, MULT)
+
+            p_t_psum = psum_two.tile([P, TB, P], BF16, name="p_t_psum", tag="turned")
             for t in range(TB):
-                nc.tensor.transpose(p_t_psum[:, t, :], p_blocks[b][:, t * P : (t + 1) * P], ident[:])
+                nc.tensor.transpose(p_t_psum[:, t, :], p[:, t * P : (t + 1) * P], ident[:])
             p_t = work.tile([P, TB, P], BF16, name="p_t")
             nc.scalar.copy(p_t[:], p_t_psum[:])
 
-            o_psum = psum_two.tile([P, P], F32, name="o_psum", tag="o_psum")
+            o_psum = psum_three.tile([P, P], F32, name="o_psum", tag="o_psum")
             for t in range(TB):
                 nc.tensor.matmul(o_psum[:], v_sb[:, t, :], p_t[:, t, :], start=t == 0, stop=t == TB - 1)
             nc.vector.tensor_copy(o[:, b * P : (b + 1) * P], o_psum[:])
+
+        windows = [psum_two.tile([P, S], F32, name=f"window{m}", tag="turned") for m in range(MB)]
+        for m in range(MB):
+            nc.tensor.matmul(windows[m][:], ident[:], base_sb[:, m, :], start=True, stop=False)
 
         for m in range(MB):
             nc.tensor.matmul(windows[m][:].indirect(offsets[:]), w_sb[:, m * P : (m + 1) * P], o[:],

import concourse.mybir as mybir
from concourse.masks import make_identity

BF16, F32, U16 = mybir.dt.bfloat16, mybir.dt.float32, mybir.dt.uint16
EXP = mybir.ActivationFunctionType.Exp
MAX, MULT = mybir.AluOpType.max, mybir.AluOpType.mult
AXIS_X = mybir.AxisListType.X

P = 128
S, K, M, N, T, D = 512, 128, 256, 384, 256, 128
JB, TB, MB = N // P, T // P, M // P
WARM_UPS = 5
FLOPS = 2 * (N * K * T + N * T * D + N * D * M)


def tile_rows_attnback_kernel(tc, base, q, k, v, w, r, offs, out):
    nc = tc.nc
    with (
        tc.tile_pool(name="held", bufs=1) as held,
        tc.tile_pool(name="work", bufs=JB) as work,
        tc.psum_pool(name="psum_three", bufs=JB) as psum_three,
        tc.psum_pool(name="psum_two", bufs=2) as psum_two,
    ):
        offsets = held.tile([P, N // 16], U16, name="offsets")
        base_sb = held.tile([P, MB, S], BF16, name="base_sb")
        q_sb = held.tile([P, N], BF16, name="q_sb")
        k_sb = held.tile([P, T], BF16, name="k_sb")
        v_sb = held.tile([P, TB, D], BF16, name="v_sb")
        w_sb = held.tile([P, M], BF16, name="w_sb")
        r_row = held.tile([1, T], F32, name="r_row")

        nc.sync.dma_start(r_row[:], r)
        nc.sync.dma_start(q_sb[:], q)
        nc.sync.dma_start(k_sb[:], k)
        nc.sync.dma_start(v_sb[:], v.rearrange("(a p) d -> p a d", p=P))
        nc.sync.dma_start(base_sb[:], base.rearrange("(a p) s -> p a s", p=P))
        nc.sync.dma_start(w_sb[:], w)
        nc.sync.dma_start(offsets[:], offs)

        zeros = held.tile([P, S], BF16, name="zeros")
        nc.vector.memset(zeros[:], 0.0)
        spare = psum_three.tile([P, S], F32, name="spare", tag="o_psum")
        for warm_up in range(WARM_UPS):
            nc.tensor.matmul(spare[:], zeros[:, :P], zeros[:], start=True, stop=True)

        early = held.tile([P, 1], F32, name="early")
        nc.vector.memset(early[:], 0.0)
        nc.scalar.activation(early[:], early[:], EXP)

        ones_row = held.tile([1, P], F32, name="ones_row")
        nc.vector.memset(ones_row[:], 1.0)
        ident = held.tile([P, P], BF16, name="ident")
        make_identity(nc, ident[:])

        e_blocks, totals = [], []
        for b in range(JB):
            a = psum_three.tile([P, T], F32, name="a")
            nc.tensor.matmul(a[:], ones_row[:], r_row[:], start=True, stop=False)
            nc.tensor.matmul(a[:], q_sb[:, b * P : (b + 1) * P], k_sb[:], start=False, stop=True)
            neg_max = work.tile([P, 1], F32, name="neg_max")
            nc.vector.tensor_reduce(neg_max[:], a[:], AXIS_X, MAX, negate=True)
            e = work.tile([P, T], F32, name="e")
            e_blocks.append(e)
            total = work.tile([P, 1], F32, name="total")
            nc.scalar.activation(e[:], a[:], EXP, bias=neg_max[:], accum_out=total[:])
            totals.append(total)

        o = held.tile([P, N], BF16, name="o")
        for b in range(JB):
            inverse = work.tile([P, 1], F32, name="inverse")
            nc.vector.reciprocal(inverse[:], totals[b][:])
            p = work.tile([P, T], BF16, name="p")
            nc.vector.tensor_scalar(p[:], e_blocks[b][:], inverse[:], None, MULT)

            p_t_psum = psum_two.tile([P, TB, P], BF16, name="p_t_psum", tag="turned")
            for t in range(TB):
                nc.tensor.transpose(p_t_psum[:, t, :], p[:, t * P : (t + 1) * P], ident[:])
            p_t = work.tile([P, TB, P], BF16, name="p_t")
            nc.scalar.copy(p_t[:], p_t_psum[:])

            o_psum = psum_three.tile([P, P], F32, name="o_psum", tag="o_psum")
            for t in range(TB):
                nc.tensor.matmul(o_psum[:], v_sb[:, t, :], p_t[:, t, :], start=t == 0, stop=t == TB - 1)
            nc.vector.tensor_copy(o[:, b * P : (b + 1) * P], o_psum[:])

        windows = [psum_two.tile([P, S], F32, name=f"window{m}", tag="turned") for m in range(MB)]
        for m in range(MB):
            nc.tensor.matmul(windows[m][:], ident[:], base_sb[:, m, :], start=True, stop=False)

        for m in range(MB):
            nc.tensor.matmul(windows[m][:].indirect(offsets[:]), w_sb[:, m * P : (m + 1) * P], o[:],
                             start=False, stop=True)

        for m in range(MB):
            z = held.tile([P, S], F32, name=f"z{m}")
            if m == 0:
                nc.vector.tensor_copy(z[:], windows[m][:])
            else:
                nc.scalar.copy(z[:], windows[m][:])
            nc.sync.dma_start(out[m * P : (m + 1) * P, :], z[:])
